import numpy as np
CORES = [7,135,263,391,15,143,271,399,23,151,279,407,31,159,287,415]
N = 16
ROWS, COLS = 4, 4
def setup_inputs(rng):
    return {"x": rng.standard_normal((N, 128, 256), dtype=np.float32)}
def reference(x):
    g = x.astype(np.float64).reshape(ROWS, COLS, 128, 256)
    rs = g.sum(axis=1)
    cs = g.sum(axis=0)
    y1 = np.stack([rs[r // COLS] for r in range(N)]).astype(x.dtype)
    y2 = np.stack([cs[r % COLS] for r in range(N)]).astype(x.dtype)
    return {"y1": y1, "y2": y2}

@@ -1,0 +1,82 @@
+from concourse.bass import DstId, RemoteDMATransfer
+from concourse.mybir import AluOpType
+
+W = 256
+H = W // 2
+
+SCRATCH = {
+    "xs": ("sbuf", [128, W], "float32"),
+    "r1": ("sbuf", [128, H], "float32"),
+    "r2": ("sbuf", [128, H], "float32"),
+    "r3": ("sbuf", [128, H], "float32"),
+    "c1": ("sbuf", [128, H], "float32"),
+    "c2": ("sbuf", [128, H], "float32"),
+    "c3": ("sbuf", [128, H], "float32"),
+}
+SEMAPHORES = ["ld", "i1", "i2", "ar1", "ar2", "ar3", "ac1", "ac2", "ac3", "sent", "acc1", "acc2", "st"]
+
+OFFCHIP = 0x00FF
+NE = 8
+
+
+def rank_program(g, core, T, topo):
+    if T.rank_of(core) is None:
+        return
+    S = T.sem
+    h, c = topo.host(core), topo.chip(core)
+
+    def at(host, chip):
+        return host * 128 + chip * 8 + core % 8
+
+    row_near, row_far = at(h ^ 1, c), at(3 - h, c)
+    col_near, col_far = at(h, c ^ 1), at(h, c ^ 2)
+    rk = 0 if h in (0, 3) else 1
+    ck = c & 1
+
+    def half(t, k):
+        return t[:, k * H:(k + 1) * H]
+
+    def send(dst, out, srcs, sem):
+        rid, pid = topo.addr(dst, core)
+        if len(srcs) == 1:
+            g.remote_dma(out[:], srcs[0], sem, S.sent, pid, rid, OFFCHIP)
+        else:
+            g.remote_dma_fused([RemoteDMATransfer(dst_ids=[DstId(rid=rid, pnc=pid)], dma_engine_mask=OFFCHIP,
+                                                  remote_sem=sem, srcs=srcs, dsts=[out[:]], alu_op=1)],
+                               local_sem=S.sent)
+
+    g.sync.dma_start(T.xs[:], T.x[:]).then_inc(S.ld, 16)
+    g.scalar.dma_start(half(T.y1, rk), half(T.x, rk)).then_inc(S.i1, 16)
+    g.scalar.dma_start(half(T.y2, ck), half(T.x, ck)).then_inc(S.i2, 16)
+
+    g.wait_ge(S.ld, 16)
+    send(row_near, T.r1, [half(T.xs, 1 - rk)], S.ar1)
+    send(col_near, T.c1, [half(T.xs, 1 - ck)], S.ac1)
+
+    g.wait_ge(S.ar1, NE)
+    send(row_far, T.r2, [half(T.xs, rk), T.r1[:]], S.ar2)
+    g.wait_ge(S.ac1, NE)
+    send(col_far, T.c2, [half(T.xs, ck), T.c1[:]], S.ac2)
+    g.wait_ge(S.i1, 16)
+    g.dma_start(half(T.y1, rk), T.r1[:], accum_op=AluOpType.add).then_inc(S.acc1, 16)
+    g.wait_ge(S.i2, 16)
+    g.dma_start(half(T.y2, ck), T.c1[:], accum_op=AluOpType.add).then_inc(S.acc2, 16)
+
+    g.wait_ge(S.ar2, NE)
+    send(row_near, T.r3, [half(T.xs, rk), T.r1[:], T.r2[:]], S.ar3)
+    g.wait_ge(S.ac2, NE)
+    send(col_near, T.c3, [half(T.xs, ck), T.c1[:], T.c2[:]], S.ac3)
+    g.wait_ge(S.acc1, 16)
+    g.dma_start(half(T.y1, rk), T.r2[:], accum_op=AluOpType.add).then_inc(S.acc1, 16)
+    g.wait_ge(S.acc2, 16)
+    g.dma_start(half(T.y2, ck), T.c2[:], accum_op=AluOpType.add).then_inc(S.acc2, 16)
+
+    g.sync.wait_ge(S.ar3, NE)
+    g.sync.dma_start(half(T.y1, 1 - rk), T.r3[:]).then_inc(S.st, 16)
+    g.scalar.wait_ge(S.ac3, NE)
+    g.scalar.dma_start(half(T.y2, 1 - ck), T.c3[:]).then_inc(S.st, 16)
+
+    g.wait_ge(S.acc1, 32)
+    g.wait_ge(S.acc2, 32)
+    g.wait_ge(S.sent, 6 * NE)
+    g.wait_ge(S.st, 32)

@@ -1,82 +1,86 @@
 from concourse.bass import DstId, RemoteDMATransfer
-from concourse.mybir import AluOpType
 
-W = 256
-H = W // 2
+RANK_CORE = 7
+ROW_KEEPER = (0, 2, 4, 6)
+COL_KEEPER = (3, 3, 2, 2)
+ROW_SLOT = (0, 0, 0, 0)
+COL_SLOT = (1, 2, 1, 2)
 
 SCRATCH = {
-    "xs": ("sbuf", [128, W], "float32"),
-    "r1": ("sbuf", [128, H], "float32"),
-    "r2": ("sbuf", [128, H], "float32"),
-    "r3": ("sbuf", [128, H], "float32"),
-    "c1": ("sbuf", [128, H], "float32"),
-    "c2": ("sbuf", [128, H], "float32"),
-    "c3": ("sbuf", [128, H], "float32"),
+    "xd": ("dram", [8, 128, 32], "float32"),
+    "h1": ("dram", [3, 128, 32], "float32"),
+    "h2": ("dram", [3, 128, 32], "float32"),
+    "s1": ("dram", [8, 128, 32], "float32"),
+    "s2": ("dram", [8, 128, 32], "float32"),
 }
-SEMAPHORES = ["ld", "i1", "i2", "ar1", "ar2", "ar3", "ac1", "ac2", "ac3", "sent", "acc1", "acc2", "st"]
+SEMAPHORES = ["ld", "r1", "r2", "r3", "c1", "c2", "c3", "sent", "st"]
 
-OFFCHIP = 0x00FF
-NE = 8
+OFFCHIP_ENGINES = 8
 
 
 def rank_program(g, core, T, topo):
-    if T.rank_of(core) is None:
+    h, c, k = topo.host(core), topo.chip(core), core % 8
+    if c > 3:
         return
     S = T.sem
-    h, c = topo.host(core), topo.chip(core)
 
-    def at(host, chip):
-        return host * 128 + chip * 8 + core % 8
+    def at(host, chip, idx):
+        return host * 128 + chip * 8 + idx
 
-    row_near, row_far = at(h ^ 1, c), at(3 - h, c)
-    col_near, col_far = at(h, c ^ 1), at(h, c ^ 2)
-    rk = 0 if h in (0, 3) else 1
-    ck = c & 1
+    def dst(d):
+        rid, pid = topo.addr(d, core)
+        return DstId(rid=rid, pnc=pid)
 
-    def half(t, k):
-        return t[:, k * H:(k + 1) * H]
+    row = {"near": (h ^ 1, c), "far": (3 - h, c), "keep": 0 if h in (0, 3) else 1,
+           "keeper": ROW_KEEPER, "slot": ROW_SLOT, "a1": S.r1, "a2": S.r2, "a3": S.r3, "sum": T.s1}
+    col = {"near": (h, c ^ 1), "far": (h, c ^ 2), "keep": c & 1,
+           "keeper": COL_KEEPER, "slot": COL_SLOT, "a1": S.c1, "a2": S.c2, "a3": S.c3, "sum": T.s2}
 
-    def send(dst, out, srcs, sem):
-        rid, pid = topo.addr(dst, core)
-        if len(srcs) == 1:
-            g.remote_dma(out[:], srcs[0], sem, S.sent, pid, rid, OFFCHIP)
-        else:
-            g.remote_dma_fused([RemoteDMATransfer(dst_ids=[DstId(rid=rid, pnc=pid)], dma_engine_mask=OFFCHIP,
-                                                  remote_sem=sem, srcs=srcs, dsts=[out[:]], alu_op=1)],
-                               local_sem=S.sent)
+    if k == RANK_CORE:
+        g.sync.dma_start(T.xd[:], T.x[:]).then_inc(S.ld, 16)
+        g.wait_ge(S.ld, 16)
+        out, stay = [], []
+        for m in (row, col):
+            for q in range(4):
+                mine, theirs = 4 * m["keep"] + q, 4 * (1 - m["keep"]) + q
+                out.append(RemoteDMATransfer(dst_ids=[dst(at(m["near"][0], m["near"][1], m["keeper"][q]))],
+                                             dma_engine_mask=1 << len(out), remote_sem=m["a1"],
+                                             src=T.xd[theirs], dst=T.h1[m["slot"][q]]))
+                stay.append(RemoteDMATransfer(dst_ids=[dst(at(h, c, m["keeper"][q]))],
+                                              dma_engine_mask=1 << (OFFCHIP_ENGINES + len(stay)), remote_sem=m["a1"],
+                                              src=T.xd[mine], dst=T.xd[mine]))
+        g.remote_dma_fused(out + stay, local_sem=S.sent)
+        g.sync.wait_ge(S.r3, 8 * OFFCHIP_ENGINES)
+        g.sync.dma_start(T.y1[:], T.s1[:]).then_inc(S.st, 16)
+        g.scalar.wait_ge(S.c3, 4 * OFFCHIP_ENGINES)
+        g.scalar.dma_start(T.y2[:], T.s2[:]).then_inc(S.st, 16)
+        g.wait_ge(S.sent, 16)
+        g.wait_ge(S.st, 32)
+        return
 
-    g.sync.dma_start(T.xs[:], T.x[:]).then_inc(S.ld, 16)
-    g.scalar.dma_start(half(T.y1, rk), half(T.x, rk)).then_inc(S.i1, 16)
-    g.scalar.dma_start(half(T.y2, ck), half(T.x, ck)).then_inc(S.i2, 16)
+    jobs = [(m, [q for q in range(4) if m["keeper"][q] == k]) for m in (row, col)]
+    jobs = [(m, qs) for m, qs in jobs if qs]
+    if not jobs:
+        return
 
-    g.wait_ge(S.ld, 16)
-    send(row_near, T.r1, [half(T.xs, 1 - rk)], S.ar1)
-    send(col_near, T.c1, [half(T.xs, 1 - ck)], S.ac1)
+    def fold(qs, srcs_of, dsts_of, sem):
+        ne = OFFCHIP_ENGINES // len(qs)
+        g.remote_dma_fused([RemoteDMATransfer(dst_ids=[dst(p[0]) for p in dsts_of(q)],
+                                              dma_engine_mask=((1 << ne) - 1) << (i * ne), remote_sem=sem,
+                                              srcs=srcs_of(q), dsts=[p[1] for p in dsts_of(q)], alu_op=1)
+                            for i, q in enumerate(qs)], local_sem=S.sent)
 
-    g.wait_ge(S.ar1, NE)
-    send(row_far, T.r2, [half(T.xs, rk), T.r1[:]], S.ar2)
-    g.wait_ge(S.ac1, NE)
-    send(col_far, T.c2, [half(T.xs, ck), T.c1[:]], S.ac2)
-    g.wait_ge(S.i1, 16)
-    g.dma_start(half(T.y1, rk), T.r1[:], accum_op=AluOpType.add).then_inc(S.acc1, 16)
-    g.wait_ge(S.i2, 16)
-    g.dma_start(half(T.y2, ck), T.c1[:], accum_op=AluOpType.add).then_inc(S.acc2, 16)
-
-    g.wait_ge(S.ar2, NE)
-    send(row_near, T.r3, [half(T.xs, rk), T.r1[:], T.r2[:]], S.ar3)
-    g.wait_ge(S.ac2, NE)
-    send(col_near, T.c3, [half(T.xs, ck), T.c1[:], T.c2[:]], S.ac3)
-    g.wait_ge(S.acc1, 16)
-    g.dma_start(half(T.y1, rk), T.r2[:], accum_op=AluOpType.add).then_inc(S.acc1, 16)
-    g.wait_ge(S.acc2, 16)
-    g.dma_start(half(T.y2, ck), T.c2[:], accum_op=AluOpType.add).then_inc(S.acc2, 16)
-
-    g.sync.wait_ge(S.ar3, NE)
-    g.sync.dma_start(half(T.y1, 1 - rk), T.r3[:]).then_inc(S.st, 16)
-    g.scalar.wait_ge(S.ac3, NE)
-    g.scalar.dma_start(half(T.y2, 1 - ck), T.c3[:]).then_inc(S.st, 16)
-
-    g.wait_ge(S.acc1, 32)
-    g.wait_ge(S.acc2, 32)
-    g.wait_ge(S.sent, 6 * NE)
-    g.wait_ge(S.st, 32)
+    for m, qs in jobs:
+        g.wait_ge(m["a1"], 2 * len(qs))
+        fold(qs,
+             lambda q: [T.xd[4 * m["keep"] + q], T.h1[m["slot"][q]]],
+             lambda q: [(at(m["far"][0], m["far"][1], k), T.h2[m["slot"][q]])],
+             m["a2"])
+    for m, qs in jobs:
+        g.wait_ge(m["a2"], OFFCHIP_ENGINES)
+        fold(qs,
+             lambda q: [T.xd[4 * m["keep"] + q], T.h1[m["slot"][q]], T.h2[m["slot"][q]]],
+             lambda q: [(at(m["near"][0], m["near"][1], RANK_CORE), m["sum"][4 * m["keep"] + q]),
+                        (at(h, c, RANK_CORE), m["sum"][4 * m["keep"] + q])],
+             m["a3"])
+    g.wait_ge(S.sent, 2 * len(jobs) * OFFCHIP_ENGINES)

from concourse.bass import DstId, RemoteDMATransfer

RANK_CORE = 7
ROW_KEEPER = (0, 2, 4, 6)
COL_KEEPER = (3, 3, 2, 2)
ROW_SLOT = (0, 0, 0, 0)
COL_SLOT = (1, 2, 1, 2)

SCRATCH = {
    "xd": ("dram", [8, 128, 32], "float32"),
    "h1": ("dram", [3, 128, 32], "float32"),
    "h2": ("dram", [3, 128, 32], "float32"),
    "s1": ("dram", [8, 128, 32], "float32"),
    "s2": ("dram", [8, 128, 32], "float32"),
}
SEMAPHORES = ["ld", "r1", "r2", "r3", "c1", "c2", "c3", "sent", "st"]

OFFCHIP_ENGINES = 8


def rank_program(g, core, T, topo):
    h, c, k = topo.host(core), topo.chip(core), core % 8
    if c > 3:
        return
    S = T.sem

    def at(host, chip, idx):
        return host * 128 + chip * 8 + idx

    def dst(d):
        rid, pid = topo.addr(d, core)
        return DstId(rid=rid, pnc=pid)

    row = {"near": (h ^ 1, c), "far": (3 - h, c), "keep": 0 if h in (0, 3) else 1,
           "keeper": ROW_KEEPER, "slot": ROW_SLOT, "a1": S.r1, "a2": S.r2, "a3": S.r3, "sum": T.s1}
    col = {"near": (h, c ^ 1), "far": (h, c ^ 2), "keep": c & 1,
           "keeper": COL_KEEPER, "slot": COL_SLOT, "a1": S.c1, "a2": S.c2, "a3": S.c3, "sum": T.s2}

    if k == RANK_CORE:
        g.sync.dma_start(T.xd[:], T.x[:]).then_inc(S.ld, 16)
        g.wait_ge(S.ld, 16)
        out, stay = [], []
        for m in (row, col):
            for q in range(4):
                mine, theirs = 4 * m["keep"] + q, 4 * (1 - m["keep"]) + q
                out.append(RemoteDMATransfer(dst_ids=[dst(at(m["near"][0], m["near"][1], m["keeper"][q]))],
                                             dma_engine_mask=1 << len(out), remote_sem=m["a1"],
                                             src=T.xd[theirs], dst=T.h1[m["slot"][q]]))
                stay.append(RemoteDMATransfer(dst_ids=[dst(at(h, c, m["keeper"][q]))],
                                              dma_engine_mask=1 << (OFFCHIP_ENGINES + len(stay)), remote_sem=m["a1"],
                                              src=T.xd[mine], dst=T.xd[mine]))
        g.remote_dma_fused(out + stay, local_sem=S.sent)
        g.sync.wait_ge(S.r3, 8 * OFFCHIP_ENGINES)
        g.sync.dma_start(T.y1[:], T.s1[:]).then_inc(S.st, 16)
        g.scalar.wait_ge(S.c3, 4 * OFFCHIP_ENGINES)
        g.scalar.dma_start(T.y2[:], T.s2[:]).then_inc(S.st, 16)
        g.wait_ge(S.sent, 16)
        g.wait_ge(S.st, 32)
        return

    jobs = [(m, [q for q in range(4) if m["keeper"][q] == k]) for m in (row, col)]
    jobs = [(m, qs) for m, qs in jobs if qs]
    if not jobs:
        return

    def fold(qs, srcs_of, dsts_of, sem):
        ne = OFFCHIP_ENGINES // len(qs)
        g.remote_dma_fused([RemoteDMATransfer(dst_ids=[dst(p[0]) for p in dsts_of(q)],
                                              dma_engine_mask=((1 << ne) - 1) << (i * ne), remote_sem=sem,
                                              srcs=srcs_of(q), dsts=[p[1] for p in dsts_of(q)], alu_op=1)
                            for i, q in enumerate(qs)], local_sem=S.sent)

    for m, qs in jobs:
        g.wait_ge(m["a1"], 2 * len(qs))
        fold(qs,
             lambda q: [T.xd[4 * m["keep"] + q], T.h1[m["slot"][q]]],
             lambda q: [(at(m["far"][0], m["far"][1], k), T.h2[m["slot"][q]])],
             m["a2"])
    for m, qs in jobs:
        g.wait_ge(m["a2"], OFFCHIP_ENGINES)
        fold(qs,
             lambda q: [T.xd[4 * m["keep"] + q], T.h1[m["slot"][q]], T.h2[m["slot"][q]]],
             lambda q: [(at(m["near"][0], m["near"][1], RANK_CORE), m["sum"][4 * m["keep"] + q]),
                        (at(h, c, RANK_CORE), m["sum"][4 * m["keep"] + q])],
             m["a3"])
    g.wait_ge(S.sent, 2 * len(jobs) * OFFCHIP_ENGINES)
